import numpy as np
import ml_dtypes


def mxq(x, axis, fmt="e4m3"):
    dtype, down = {"e4m3": (ml_dtypes.float8_e4m3fn, 7), "e5m2": (ml_dtypes.float8_e5m2, 14)}[fmt]
    v = np.moveaxis(np.asarray(x, np.float32).astype(ml_dtypes.bfloat16).astype(np.float64), axis, -1)
    blocks = v.reshape(v.shape[:-1] + (-1, 32))
    amax = np.abs(blocks).max(-1, keepdims=True)
    byte = np.maximum(np.where(amax > 0, np.frexp(amax)[1] - 1 + 127, 0) - down, 1)
    scale = np.exp2(byte - 127.0)
    codes = (blocks / scale).astype(np.float32).astype(dtype).astype(np.float64)
    return np.moveaxis((codes * scale).reshape(v.shape), -1, axis)


WIDE = False


def mx_kscale(k):
    if not WIDE:
        return np.ones(k)
    levels = np.array([10, -10, 5, -5, 0])
    if k % 512:
        return np.exp2(np.random.permutation(np.resize(levels, k // 32))).repeat(32)
    a = np.empty((k // 512, 16))
    for p in range(k // 512):
        a[p, :8] = np.random.permutation(np.resize(levels, 8))
        for g in range(8):
            far = levels[np.abs(levels - a[p, g]) >= 10]
            a[p, g + 8] = far[np.random.randint(len(far))]
    return np.exp2(a.ravel()).repeat(32)


BF16 = ml_dtypes.bfloat16


def bf(x):
    return np.asarray(x, np.float32).astype(BF16)


def f64(x):
    return np.asarray(x).astype(np.float64)


T, D, F, E = 1536, 1024, 512, 1024


def draw0():
    sq, sk, sv = mx_kscale(D), mx_kscale(D), mx_kscale(D)
    u = mx_kscale(F)
    r = mx_kscale(T)
    return {
        "xq": bf(np.random.standard_normal((T, D)) * sq),
        "xk": bf(np.random.standard_normal((T, D)) * sk * r[:, None]),
        "xv": bf(np.random.standard_normal((T, D)) * sv / r[:, None]),
        "wq": bf(np.random.standard_normal((D, F)) / np.sqrt(D) / F ** 0.25 / sq[:, None] * u),
        "wk": bf(np.random.standard_normal((D, F)) / np.sqrt(D) / T ** 0.25 / sk[:, None]),
        "wv": bf(np.random.standard_normal((D, E)) / np.sqrt(D) / T ** 0.25 / sv[:, None]),
        "state": bf(np.random.standard_normal((F, E)) / u[:, None]),
        "decay": bf(np.random.uniform(0.4, 0.9, F) * u),
    }


def core(xq, xk, xv, wq, wk, wv, state, decay):
    st = f64(state)
    q = mxq(f64(xq), 1, "e4m3") @ mxq(f64(wq), 0, "e4m3")
    k = mxq(f64(xk), 1, "e4m3") @ mxq(f64(wk), 0, "e4m3")
    v = mxq(f64(xv), 1, "e4m3") @ mxq(f64(wv), 0, "e4m3")
    k = np.maximum(k, 0.0)
    o = mxq(q, 1, "e4m3") @ mxq(st, 0, "e4m3")
    upd = mxq(k, 0, "e4m3").T @ mxq(v, 0, "e4m3")
    new_state = f64(decay)[:, None] * st + upd
    return o, new_state


def e4m3fn_bytes(y):
    return np.clip(np.asarray(y, np.float64), -448.0, 448.0).astype(np.float32).astype(ml_dtypes.float8_e4m3fn).view(np.uint8)


def e4m3fn_values(b):
    return np.asarray(b, np.uint8).view(ml_dtypes.float8_e4m3fn).astype(np.float64)


def setup_inputs():
    d = draw0()
    x0 = np.asarray(d['xq']).astype(np.float64)
    s = (np.max(np.abs(x0), axis=(0,), keepdims=True) / 448.0).astype(np.float32)
    out = {}
    for k, v in d.items():
        if k == 'xq':
            out['xq_bytes'] = e4m3fn_bytes(x0 / s.astype(np.float64))
            out['xq_scale'] = s
        else:
            out[k] = v
    return out


def reference(xq_bytes, xq_scale, xk, xv, wq, wk, wv, state, decay):
    return core(e4m3fn_values(xq_bytes) * xq_scale.astype(np.float64), xk, xv, wq, wk, wv, state, decay)

@@ -1,0 +1,362 @@
+from contextlib import ExitStack
+
+import concourse.mybir as mybir
+from concourse.masks import make_identity
+
+T, D, F, E = 1536, 1024, 512, 1024
+FLOPS = 2 * T * (2 * D * F + D * E + 2 * F * E)
+
+F32 = mybir.dt.float32
+BF16 = mybir.dt.bfloat16
+U32 = mybir.dt.uint32
+U8 = mybir.dt.uint8
+FP8 = mybir.dt.float8_e4m3fn
+FP8X4 = mybir.dt.float8_e4m3fn_x4
+ACT = mybir.ActivationFunctionType
+ALU = mybir.AluOpType
+
+P = 128
+PACK = 4
+CHUNK = 512
+CHUNKS = T // CHUNK
+PASSES = D // 512
+HALF = 512
+
+
+def tile_linear_state_step_s7_kernel(
+    tc, xq_bytes, xq_scale, xk, xv, wq, wk, wv, state, decay, out_0, out_1
+):
+    nc = tc.nc
+
+    with ExitStack() as ctx:
+        sb = ctx.enter_context(tc.tile_pool(name="sb", bufs=1))
+        ps = ctx.enter_context(tc.psum_pool(name="ps", bufs=8))
+
+        ident = sb.tile([P, P], F32, name="ident", align_bytes=64)
+        make_identity(nc, ident[:])
+
+        decay_sb = sb.tile([P, PACK], BF16, name="decay_sb")
+        nc.gpsimd.dma_start(out=decay_sb[:], in_=decay.rearrange("(p i) -> p i", i=PACK))
+        warm = sb.tile([P, 1], F32, name="warm")
+        nc.vector.memset(warm[:], 0.0)
+        nc.scalar.activation(out=warm[:], in_=warm[:], func=ACT.Relu)
+
+        xdram = {"k": xk, "v": xv, "q": xq_bytes}
+        rows = {}
+        rows_q = {}
+        xcodes = {}
+
+        def load_x(kind, c, cuts=(0, 4)):
+            view = xdram[kind][c * CHUNK : (c + 1) * CHUNK, :].rearrange("(m s) d -> m s d", s=PACK)
+            if kind == "q":
+                t = sb.tile([P, PACK, D], U8, name=f"xqb{c}", tag="xq_bytes", bufs=3, align_bytes=64)
+                rows_q[c] = t
+            else:
+                t = sb.tile([P, PACK, D], BF16, name=f"x{kind}{c}", tag="x_rows", bufs=4, align_bytes=64)
+                rows[kind, c] = t
+            for a, b in zip(cuts[:-1], cuts[1:]):
+                nc.sync.dma_start(out=t[:, a:b, :], in_=view[:, a:b, :])
+
+        scale_sb = sb.tile([P, D], F32, name="scale_sb", align_bytes=64)
+        wraw = {}
+
+        def load_w(name, w):
+            width = w.shape[1]
+            for g in range(w.shape[0] // 512):
+                if name in ("wk", "wq"):
+                    t = sb.tile([P, PACK, width], BF16, name=f"{name}raw{g}", tag="w_small", bufs=2, align_bytes=64)
+                else:
+                    t = sb.tile([P, PACK, width], BF16, name=f"{name}raw{g}", align_bytes=64)
+                nc.sync.dma_start(out=t[:], in_=w[512 * g : 512 * (g + 1), :].rearrange("(p j) n -> p j n", j=PACK))
+                wraw[name, g] = t
+
+        load_x("k", 0, (0, 1, 2, 4))
+        load_w("wk", wk)
+        load_x("k", 1)
+        load_x("k", 2)
+
+        wcodes = {}
+
+        def weight_piece(name, g, h, on_scalar=False):
+            raw = wraw[name, g][:, :, h * HALF : (h + 1) * HALF]
+            grouped = sb.tile([P, HALF * PACK], BF16, name=f"{name}g{g}{h}", tag="w_grouped", bufs=3, align_bytes=64)
+            codes = sb.tile([P, HALF], U32, name=f"{name}c{g}{h}", align_bytes=64)
+            scales = sb.tile([P, HALF], U8, name=f"{name}s{g}{h}", align_bytes=64)
+            wcodes[name, g, h] = (codes, scales)
+
+            def interleave():
+                if name == "wq":
+                    nc.vector.tensor_copy(
+                        out=grouped[:].rearrange("p (t m j) -> p t m j", t=PACK, j=PACK),
+                        in_=raw.rearrange("p j (m t) -> p t m j", t=PACK),
+                    )
+                else:
+                    copy_out(
+                        grouped[:].rearrange("p (c i j) -> p c j i", i=4, j=PACK),
+                        raw.rearrange("p j (c i) -> p c j i", i=4),
+                        on_vector=not on_scalar,
+                    )
+
+            def quant():
+                nc.vector.quantize_mx(out=codes[:].bitcast(FP8X4), scales=scales[:], in_=grouped[:])
+
+            return interleave, quant
+
+        def weights(name, pieces, scalar_pieces=()):
+            made = [weight_piece(name, g, h, (g, h) in scalar_pieces) for g, h in pieces]
+            for n, (inter, _) in enumerate(made):
+                inter()
+                if n > 0:
+                    made[n - 1][1]()
+            made[-1][1]()
+
+        def copy_out(out, in_, on_vector):
+            if on_vector:
+                nc.vector.tensor_copy(out=out, in_=in_)
+            else:
+                nc.scalar.copy(out=out, in_=in_)
+
+        def load_scales():
+            nc.sync.dma_start(out=scale_sb[:], in_=xq_scale.rearrange("o k -> (o k)").partition_broadcast(P))
+
+        def product_q(c, slots):
+            if slots[0] == 0:
+                t = sb.tile([P, PACK, D], BF16, name=f"xq{c}", tag="xq_rows", bufs=2, align_bytes=64)
+                rows["q", c] = t
+            t = rows["q", c]
+            for s in slots:
+                nc.vector.tensor_tensor(
+                    out=t[:, s, :], in0=rows_q[c][:, s, :].bitcast(FP8), in1=scale_sb[:], op=ALU.mult
+                )
+
+        def transpose_unit(kind, c, on_vector=(0, 0, 0, 0)):
+            t = rows[kind, c]
+            pend = []
+            for s in range(PACK):
+                bank = ps.tile([P, 512], F32, name=f"t{kind}{c}{s}", tag="bank")
+                bank4 = bank[:].rearrange("p (g u m) -> p g u m", g=PASSES, u=2)
+                words = t[:, s, :].bitcast(F32)
+                for g in range(PASSES):
+                    for u in range(2):
+                        nc.tensor.transpose(bank4[:, g, u, :], words[:, 256 * g + u : 256 * (g + 1) : 2], ident[:])
+                grouped = sb.tile([P, PASSES * P * PACK], BF16, name=f"g{kind}{c}{s}", tag="x_grouped", bufs=6, align_bytes=64)
+                copy_out(
+                    grouped[:].bitcast(F32).rearrange("p (g m u) -> p g m u", g=PASSES, u=2),
+                    bank4.rearrange("p g u m -> p g m u"),
+                    on_vector=on_vector[s],
+                )
+                codes = sb.tile([P, PASSES * P], U32, name=f"c{kind}{c}{s}", tag="x_codes", bufs=12, align_bytes=64)
+                scales = sb.tile([P, PASSES * P], U8, name=f"s{kind}{c}{s}", tag="x_scales", bufs=12, align_bytes=64)
+                xcodes[kind, c, s] = (codes, scales)
+                pend.append((codes, scales, grouped))
+                if s > 0:
+                    quant_x(*pend[s - 1])
+            quant_x(*pend[PACK - 1])
+
+        def quant_x(codes, scales, grouped):
+            nc.vector.quantize_mx(out=codes[:].bitcast(FP8X4), scales=scales[:], in_=grouped[:])
+
+        def x_operand(kind, c, s, g):
+            codes, scales = xcodes[kind, c, s]
+            cols = slice(g * P, (g + 1) * P)
+            return codes[:, cols].bitcast(FP8X4), scales[:, cols]
+
+        def w_operand(name, g, h, a, b):
+            codes, scales = wcodes[name, g, h]
+            return codes[:, a:b].bitcast(FP8X4), scales[:, a:b]
+
+        kcodes, vcodes, qcodes = {}, {}, {}
+
+        def new_operand(name, words, tag, bufs):
+            codes = sb.tile([P, words], U32, name=f"{name}_codes", tag=f"{tag}_codes", bufs=bufs, align_bytes=64)
+            scales = sb.tile([P, words], U8, name=f"{name}_scales", tag=f"{tag}_scales", bufs=bufs, align_bytes=64)
+            return codes, scales
+
+        def grouped_tile(name):
+            return sb.tile([P, 2048], BF16, name=name, tag="y_grouped", bufs=4, align_bytes=64)
+
+        def project_k(c):
+            grouped = grouped_tile(f"kg{c}")
+            kcodes[c] = new_operand(f"k{c}", F, "k", 3)
+
+            def fill(q):
+                bank = ps.tile([P, 512], F32, name=f"kb{c}{q}", tag="bank")
+                for s in range(PACK):
+                    for g in range(PASSES):
+                        lhs, lhs_s = x_operand("k", c, s, g)
+                        rhs, rhs_s = w_operand("wk", g, 0, q * P, (q + 1) * P)
+                        nc.tensor.matmul_mx(
+                            out=bank[:, s * P : (s + 1) * P], lhsT=lhs, lhsT_scale=lhs_s, rhs=rhs, rhs_scale=rhs_s,
+                            start=(g == 0), stop=(g == PASSES - 1),
+                        )
+                nc.scalar.activation(
+                    out=grouped[:].rearrange("p (i m s) -> p i m s", i=PACK, s=PACK)[:, :, 32 * q : 32 * q + 32, :],
+                    in_=bank[:].rearrange("p (s m i) -> p i m s", s=PACK, i=PACK),
+                    func=ACT.Relu,
+                )
+                if q == 3:
+                    codes, scales = kcodes[c]
+                    nc.vector.quantize_mx(out=codes[:].bitcast(FP8X4), scales=scales[:], in_=grouped[:])
+
+            return [(fill, q) for q in range(4)]
+
+        def project_v(c):
+            halves = {}
+
+            def fill(n):
+                h, q = n // 4, n % 4
+                if q == 0:
+                    grouped = grouped_tile(f"vg{c}{h}")
+                    halves[h] = grouped
+                    vcodes[c, h] = new_operand(f"v{c}{h}", HALF, "v", 6)
+                grouped = halves[h]
+                if True:
+                    bank = ps.tile([P, 512], F32, name=f"vb{c}{h}{q}", tag="bank")
+                    for s in range(PACK):
+                        for g in range(PASSES):
+                            lhs, lhs_s = x_operand("v", c, s, g)
+                            rhs, rhs_s = w_operand("wv", g, h, q * P, (q + 1) * P)
+                            nc.tensor.matmul_mx(
+                                out=bank[:, s * P : (s + 1) * P], lhsT=lhs, lhsT_scale=lhs_s, rhs=rhs, rhs_scale=rhs_s,
+                                start=(g == 0), stop=(g == PASSES - 1),
+                            )
+                    copy_out(
+                        grouped[:].rearrange("p (n s) -> p n s", s=PACK)[:, q * P : (q + 1) * P, :],
+                        bank[:].rearrange("p (s n) -> p n s", s=PACK),
+                        on_vector=(q == 3),
+                    )
+                if q == 3:
+                    codes, scales = vcodes[c, h]
+                    nc.vector.quantize_mx(out=codes[:].bitcast(FP8X4), scales=scales[:], in_=grouped[:])
+
+            return [(fill, n) for n in range(8)]
+
+        def project_q(c):
+            grouped = grouped_tile(f"qg{c}")
+
+            def fill(s):
+                bank = ps.tile([P, 512], F32, name=f"qb{c}{s}", tag="bank")
+                for j in range(PACK):
+                    for g in range(PASSES):
+                        lhs, lhs_s = w_operand("wq", g, 0, j * P, (j + 1) * P)
+                        rhs, rhs_s = x_operand("q", c, s, g)
+                        nc.tensor.matmul_mx(
+                            out=bank[:, j * P : (j + 1) * P], lhsT=lhs, lhsT_scale=lhs_s, rhs=rhs, rhs_scale=rhs_s,
+                            start=(g == 0), stop=(g == PASSES - 1),
+                        )
+                copy_out(
+                    grouped[:, s * 512 : (s + 1) * 512].rearrange("p (m j) -> p m j", j=PACK),
+                    bank[:].rearrange("p (j m) -> p m j", j=PACK),
+                    on_vector=False,
+                )
+                if s % 2 == 1:
+                    pair = s // 2
+                    qcodes[c, pair] = new_operand(f"q{c}{pair}", 2 * P, "q", 4)
+                    codes, scales = qcodes[c, pair]
+                    nc.vector.quantize_mx(
+                        out=codes[:].bitcast(FP8X4), scales=scales[:], in_=grouped[:, pair * 1024 : (pair + 1) * 1024]
+                    )
+
+            return [(fill, s) for s in range(PACK)]
+
+        out_view = out_0.rearrange("(c m s) e -> c m s e", m=P, s=PACK)
+
+        def read_state(c):
+            row_tiles = {}
+
+            def fill(n):
+                s, h = n // 2, n % 2
+                codes, scales = qcodes[c, s // 2]
+                cols = slice((s % 2) * P, (s % 2 + 1) * P)
+                if h == 0:
+                    o_sb = sb.tile([P, E], F32, name=f"o{c}{s}", tag="out_rows", bufs=4)
+                    row_tiles[s] = o_sb
+                o_sb = row_tiles[s]
+                if True:
+                    bank = ps.tile([P, 512], F32, name=f"ob{c}{s}{h}", tag="bank")
+                    rhs, rhs_s = w_operand("st", 0, h, 0, HALF)
+                    nc.tensor.matmul_mx(
+                        out=bank[:], lhsT=codes[:, cols].bitcast(FP8X4), lhsT_scale=scales[:, cols],
+                        rhs=rhs, rhs_scale=rhs_s, start=True, stop=True,
+                    )
+                    copy_out(o_sb[:, h * HALF : (h + 1) * HALF], bank[:], on_vector=(h == 1 and s % 2 == 1))
+                if h == 1:
+                    nc.sync.dma_start(out=out_view[c, :, s, :], in_=o_sb[:])
+
+            return [(fill, n) for n in range(8)]
+
+        new_view = out_1.rearrange("(p i) e -> p i e", i=PACK)
+
+        def update_state(h):
+            banks = {}
+
+            def passes(i, chunks):
+                for c in chunks:
+                    codes, scales = kcodes[c]
+                    vc, vs = vcodes[c, h]
+                    cols = slice(i * P, (i + 1) * P)
+                    nc.tensor.matmul_mx(
+                        out=banks[i][:], lhsT=codes[:, cols].bitcast(FP8X4), lhsT_scale=scales[:, cols],
+                        rhs=vc[:].bitcast(FP8X4), rhs_scale=vs[:], start=(c == 0), stop=(c == 2),
+                    )
+
+            def fill(i):
+                bank = ps.tile([P, 512], F32, name=f"ub{h}{i}", tag="bank")
+                banks[i] = bank
+                passes(i, (0, 1, 2))
+                new_sb = sb.tile([P, HALF], F32, name=f"n{h}{i}", tag="new_rows", bufs=3)
+                cut = slice(h * HALF, (h + 1) * HALF)
+                nc.vector.scalar_tensor_tensor(
+                    out=new_sb[:], in0=wraw["st", 0][:, i, cut], scalar=decay_sb[:, i : i + 1], in1=bank[:],
+                    op0=ALU.mult, op1=ALU.add,
+                )
+                nc.sync.dma_start(out=new_view[:, i, cut], in_=new_sb[:])
+
+            return [(fill, i) for i in range(PACK)]
+
+        def run(*lists):
+            for n in range(max(len(x) for x in lists)):
+                for x in lists:
+                    if n < len(x):
+                        fill, arg = x[n]
+                        fill(arg)
+
+        with tc.manual_schedule(engines={mybir.EngineType.PE}):
+            transpose_unit("k", 0)
+            weights("wk", ((0, 0), (1, 0)), ((1, 0),))
+            transpose_unit("k", 1)
+            load_w("wv", wv)
+            load_x("v", 0)
+            load_x("v", 1)
+            load_scales()
+            load_x("q", 0)
+            run(project_k(0))
+            weights("wv", ((0, 0), (1, 0)))
+            transpose_unit("k", 2)
+            load_w("wq", wq)
+            load_x("q", 1)
+            load_w("st", state)
+            load_x("v", 2)
+            load_x("q", 2)
+            run(project_k(1))
+            weights("wv", ((0, 1), (1, 1)))
+            transpose_unit("v", 0)
+            run(project_k(2))
+            weights("wq", ((0, 0), (1, 0)))
+            product_q(0, (0, 1, 2, 3))
+            transpose_unit("v", 1)
+            run(project_v(0))
+            product_q(1, (0, 1, 2, 3))
+            transpose_unit("q", 0)
+            run(project_v(1))
+            weights("st", ((0, 0), (0, 1)), ((0, 1),))
+            transpose_unit("q", 1)
+            run(project_q(0))
+            product_q(2, (0, 1, 2, 3))
+            transpose_unit("v", 2)
+            run(project_q(1), read_state(0))
+            transpose_unit("q", 2)
+            run(project_v(2), read_state(1))
+            run(project_q(2))
+            run(update_state(0))
+            run(read_state(2), update_state(1))

@@ -36,7 +36,6 @@ def tile_linear_state_step_s7_kernel(
         make_identity(nc, ident[:])
 
         decay_sb = sb.tile([P, PACK], BF16, name="decay_sb")
-        nc.gpsimd.dma_start(out=decay_sb[:], in_=decay.rearrange("(p i) -> p i", i=PACK))
         warm = sb.tile([P, 1], F32, name="warm")
         nc.vector.memset(warm[:], 0.0)
         nc.scalar.activation(out=warm[:], in_=warm[:], func=ACT.Relu)
@@ -104,11 +103,7 @@ def tile_linear_state_step_s7_kernel(
 
         def weights(name, pieces, scalar_pieces=()):
             made = [weight_piece(name, g, h, (g, h) in scalar_pieces) for g, h in pieces]
-            for n, (inter, _) in enumerate(made):
-                inter()
-                if n > 0:
-                    made[n - 1][1]()
-            made[-1][1]()
+            return [x for x, _ in made] + [x for _, x in made]
 
         def copy_out(out, in_, on_vector):
             if on_vector:
@@ -119,20 +114,20 @@ def tile_linear_state_step_s7_kernel(
         def load_scales():
             nc.sync.dma_start(out=scale_sb[:], in_=xq_scale.rearrange("o k -> (o k)").partition_broadcast(P))
 
-        def product_q(c, slots):
-            if slots[0] == 0:
-                t = sb.tile([P, PACK, D], BF16, name=f"xq{c}", tag="xq_rows", bufs=2, align_bytes=64)
-                rows["q", c] = t
-            t = rows["q", c]
-            for s in slots:
+        def product_q(c):
+            def slot(s):
+                if s == 0:
+                    rows["q", c] = sb.tile([P, PACK, D], BF16, name=f"xq{c}", tag="xq_rows", bufs=2, align_bytes=64)
                 nc.vector.tensor_tensor(
-                    out=t[:, s, :], in0=rows_q[c][:, s, :].bitcast(FP8), in1=scale_sb[:], op=ALU.mult
+                    out=rows["q", c][:, s, :], in0=rows_q[c][:, s, :].bitcast(FP8), in1=scale_sb[:], op=ALU.mult
                 )
 
-        def transpose_unit(kind, c, on_vector=(0, 0, 0, 0)):
+            return [lambda: slot(0), lambda: slot(1), lambda: slot(2), lambda: slot(3)]
+
+        def transpose_unit(kind, c, slots=(0, 1, 2, 3), on_vector=(0, 0, 0, 0)):
             t = rows[kind, c]
             pend = []
-            for s in range(PACK):
+            for s in slots:
                 bank = ps.tile([P, 512], F32, name=f"t{kind}{c}{s}", tag="bank")
                 bank4 = bank[:].rearrange("p (g u m) -> p g u m", g=PASSES, u=2)
                 words = t[:, s, :].bitcast(F32)
@@ -149,9 +144,9 @@ def tile_linear_state_step_s7_kernel(
                 scales = sb.tile([P, PASSES * P], U8, name=f"s{kind}{c}{s}", tag="x_scales", bufs=12, align_bytes=64)
                 xcodes[kind, c, s] = (codes, scales)
                 pend.append((codes, scales, grouped))
-                if s > 0:
-                    quant_x(*pend[s - 1])
-            quant_x(*pend[PACK - 1])
+                if len(pend) > 1:
+                    quant_x(*pend[-2])
+            quant_x(*pend[-1])
 
         def quant_x(codes, scales, grouped):
             nc.vector.quantize_mx(out=codes[:].bitcast(FP8X4), scales=scales[:], in_=grouped[:])
@@ -279,8 +274,11 @@ def tile_linear_state_step_s7_kernel(
                         out=bank[:], lhsT=codes[:, cols].bitcast(FP8X4), lhsT_scale=scales[:, cols],
                         rhs=rhs, rhs_scale=rhs_s, start=True, stop=True,
                     )
-                    copy_out(o_sb[:, h * HALF : (h + 1) * HALF], bank[:], on_vector=(h == 1 and s % 2 == 1))
-                if h == 1:
+                    copy_out(o_sb[:, h * HALF : (h + 1) * HALF], bank[:], on_vector=(c == 1 and h == 1))
+                if c == CHUNKS - 1:
+                    cut = slice(h * HALF, (h + 1) * HALF)
+                    nc.sync.dma_start(out=out_view[c, :, s, cut], in_=o_sb[:, cut])
+                elif h == 1:
                     nc.sync.dma_start(out=out_view[c, :, s, :], in_=o_sb[:])
 
             return [(fill, n) for n in range(8)]
@@ -304,7 +302,7 @@ def tile_linear_state_step_s7_kernel(
                 bank = ps.tile([P, 512], F32, name=f"ub{h}{i}", tag="bank")
                 banks[i] = bank
                 passes(i, (0, 1, 2))
-                new_sb = sb.tile([P, HALF], F32, name=f"n{h}{i}", tag="new_rows", bufs=3)
+                new_sb = sb.tile([P, HALF], F32, name=f"n{h}{i}", tag="new_rows", bufs=4)
                 cut = slice(h * HALF, (h + 1) * HALF)
                 nc.vector.scalar_tensor_tensor(
                     out=new_sb[:], in0=wraw["st", 0][:, i, cut], scalar=decay_sb[:, i : i + 1], in1=bank[:],
@@ -313,6 +311,22 @@ def tile_linear_state_step_s7_kernel(
                 nc.sync.dma_start(out=new_view[:, i, cut], in_=new_sb[:])
 
             return [(fill, i) for i in range(PACK)]
+
+        background = []
+
+        def work(n):
+            for _ in range(min(n, len(background))):
+                job = background[0]
+                background.remove(job)
+                job()
+
+        def spread(fills, n):
+            for i, (fill, arg) in enumerate(fills):
+                work((i + 1) * n // len(fills) - i * n // len(fills))
+                fill(arg)
+
+        def mix(a, b):
+            return [x for pair in zip(a, b) for x in pair]
 
         def run(*lists):
             for n in range(max(len(x) for x in lists)):
@@ -323,40 +337,72 @@ def tile_linear_state_step_s7_kernel(
 
         with tc.manual_schedule(engines={mybir.EngineType.PE}):
             transpose_unit("k", 0)
-            weights("wk", ((0, 0), (1, 0)), ((1, 0),))
-            transpose_unit("k", 1)
+            for job in weights("wk", ((0, 0), (1, 0)), ((1, 0),)):
+                job()
             load_w("wv", wv)
             load_x("v", 0)
             load_x("v", 1)
             load_scales()
             load_x("q", 0)
-            run(project_k(0))
-            weights("wv", ((0, 0), (1, 0)))
-            transpose_unit("k", 2)
+            background.extend(weights("wv", ((0, 0), (1, 0))))
+            background.extend(weights("wv", ((0, 1), (1, 1))))
+            background.extend(product_q(0))
+            transpose_unit("k", 1, (0, 1))
+            k = project_k(0)
+            spread(k[:2], 1)
+            transpose_unit("k", 1, (2, 3))
+            spread(k[2:], 1)
             load_w("wq", wq)
             load_x("q", 1)
             load_w("st", state)
+            nc.sync.dma_start(out=decay_sb[:], in_=decay.rearrange("(p i) -> p i", i=PACK))
             load_x("v", 2)
             load_x("q", 2)
-            run(project_k(1))
-            weights("wv", ((0, 1), (1, 1)))
-            transpose_unit("v", 0)
-            run(project_k(2))
-            weights("wq", ((0, 0), (1, 0)))
-            product_q(0, (0, 1, 2, 3))
-            transpose_unit("v", 1)
-            run(project_v(0))
-            product_q(1, (0, 1, 2, 3))
-            transpose_unit("q", 0)
-            run(project_v(1))
-            weights("st", ((0, 0), (0, 1)), ((0, 1),))
-            transpose_unit("q", 1)
-            run(project_q(0))
-            product_q(2, (0, 1, 2, 3))
-            transpose_unit("v", 2)
-            run(project_q(1), read_state(0))
-            transpose_unit("q", 2)
-            run(project_v(2), read_state(1))
-            run(project_q(2))
-            run(update_state(0))
-            run(read_state(2), update_state(1))
+            background.extend(weights("wq", ((0, 0), (1, 0))))
+            background.extend(product_q(1))
+            background.extend(weights("st", ((0, 0), (0, 1))))
+            background.extend(product_q(2))
+            transpose_unit("k", 2, (0, 1))
+            k = project_k(1)
+            spread(k[:2], 2)
+            transpose_unit("k", 2, (2, 3))
+            spread(k[2:], 3)
+            transpose_unit("v", 0, (0, 1))
+            k = project_k(2)
+            spread(k[:2], 3)
+            transpose_unit("v", 0, (2, 3))
+            spread(k[2:], 2)
+            transpose_unit("v", 1, (0, 1))
+            v = project_v(0)
+            spread(v[:4], 2)
+            transpose_unit("v", 1, (2, 3))
+            spread(v[4:], 2)
+            transpose_unit("q", 0, (0, 1))
+            v = project_v(1)
+            spread(v[:4], 3)
+            transpose_unit("q", 0, (2, 3))
+            spread(v[4:], 3)
+            transpose_unit("q", 1, (0, 1))
+            q = project_q(0)
+            spread(q[:2], 2)
+            transpose_unit("q", 1, (2, 3))
+            spread(q[2:], 2)
+            transpose_unit("v", 2, (0, 1))
+            q = project_q(1)
+            read = read_state(0)
+            spread(mix(q[:2], read[:2]) + read[2:4], 2)
+            transpose_unit("v", 2, (2, 3))
+            spread(mix(q[2:], read[4:6]) + read[6:], 2)
+            transpose_unit("q", 2, (0, 1))
+            v = project_v(2)
+            read = read_state(1)
+            run(v[:4], read[:4])
+            transpose_unit("q", 2, (2, 3))
+            run(v[4:], read[4:])
+            update = update_state(0) + update_state(1)
+            run(project_q(2), update[:2])
+            read = read_state(2)
+            run(update[2:4], read[:2])
+            run(read[2:6])
+            run(update[4:6], read[6:])
+            run(update[6:])

@@ -48,20 +48,27 @@ def tile_linear_state_step_s7_kernel(
         def load_x(kind, c, cuts=(0, 4)):
             view = xdram[kind][c * CHUNK : (c + 1) * CHUNK, :].rearrange("(m s) d -> m s d", s=PACK)
             if kind == "q":
-                t = sb.tile([P, PACK, D], U8, name=f"xqb{c}", tag="xq_bytes", bufs=3, align_bytes=64)
+                t = sb.tile([P, PACK, D], U8, name=f"xqb{c}", tag="xq_bytes", bufs=2, align_bytes=64)
                 rows_q[c] = t
             else:
-                t = sb.tile([P, PACK, D], BF16, name=f"x{kind}{c}", tag="x_rows", bufs=4, align_bytes=64)
-                rows[kind, c] = t
+                if cuts[0] == 0:
+                    rows[kind, c] = sb.tile([P, PACK, D], BF16, name=f"x{kind}{c}", tag="x_rows", bufs=4, align_bytes=64)
+                t = rows[kind, c]
             for a, b in zip(cuts[:-1], cuts[1:]):
                 nc.sync.dma_start(out=t[:, a:b, :], in_=view[:, a:b, :])
 
-        scale_sb = sb.tile([P, D], F32, name="scale_sb", align_bytes=64)
+        scale_pt = sb.tile([P, PASSES, PACK], F32, name="scale_pt", align_bytes=64)
+        ones = sb.tile([P, 1], F32, name="ones")
+        nc.vector.memset(ones[:], 1.0)
+
+        def load_scales():
+            nc.sync.dma_start(out=scale_pt[:], in_=xq_scale.rearrange("o (g p t) -> p (o g) t", p=P, t=PACK))
+
         wraw = {}
 
-        def load_w(name, w):
+        def load_w(name, w, passes=None):
             width = w.shape[1]
-            for g in range(w.shape[0] // 512):
+            for g in passes or range(w.shape[0] // 512):
                 if name in ("wk", "wq"):
                     t = sb.tile([P, PACK, width], BF16, name=f"{name}raw{g}", tag="w_small", bufs=2, align_bytes=64)
                 else:
@@ -69,30 +76,33 @@ def tile_linear_state_step_s7_kernel(
                 nc.sync.dma_start(out=t[:], in_=w[512 * g : 512 * (g + 1), :].rearrange("(p j) n -> p j n", j=PACK))
                 wraw[name, g] = t
 
-        load_x("k", 0, (0, 1, 2, 4))
-        load_w("wk", wk)
-        load_x("k", 1)
-        load_x("k", 2)
+        load_x("k", 0, (0, 2))
+        load_w("wk", wk, (0,))
+        load_x("k", 0, (2, 4))
+        load_w("wk", wk, (1,))
+        load_x("k", 1, (0, 2))
+        load_x("k", 1, (2, 4))
 
         wcodes = {}
 
-        def weight_piece(name, g, h, on_scalar=False):
-            raw = wraw[name, g][:, :, h * HALF : (h + 1) * HALF]
-            grouped = sb.tile([P, HALF * PACK], BF16, name=f"{name}g{g}{h}", tag="w_grouped", bufs=3, align_bytes=64)
-            codes = sb.tile([P, HALF], U32, name=f"{name}c{g}{h}", align_bytes=64)
-            scales = sb.tile([P, HALF], U8, name=f"{name}s{g}{h}", align_bytes=64)
-            wcodes[name, g, h] = (codes, scales)
+        def weight_piece(name, g, on_scalar=False):
+            raw = wraw[name, g]
+            width = raw.shape[2]
+            grouped = sb.tile([P, width * PACK], BF16, name=f"{name}g{g}", tag="w_grouped", bufs=2, align_bytes=64)
+            codes = sb.tile([P, width], U32, name=f"{name}c{g}", align_bytes=64)
+            scales = sb.tile([P, width], U8, name=f"{name}s{g}", align_bytes=64)
+            wcodes[name, g] = (codes, scales)
 
             def interleave():
                 if name == "wq":
                     nc.vector.tensor_copy(
                         out=grouped[:].rearrange("p (t m j) -> p t m j", t=PACK, j=PACK),
-                        in_=raw.rearrange("p j (m t) -> p t m j", t=PACK),
+                        in_=raw[:].rearrange("p j (m t) -> p t m j", t=PACK),
                     )
                 else:
                     copy_out(
                         grouped[:].rearrange("p (c i j) -> p c j i", i=4, j=PACK),
-                        raw.rearrange("p j (c i) -> p c j i", i=4),
+                        raw[:].rearrange("p j (c i) -> p c j i", i=4),
                         on_vector=not on_scalar,
                     )
 
@@ -101,8 +111,9 @@ def tile_linear_state_step_s7_kernel(
 
             return interleave, quant
 
-        def weights(name, pieces, scalar_pieces=()):
-            made = [weight_piece(name, g, h, (g, h) in scalar_pieces) for g, h in pieces]
+        def weights(name, scalar_passes=()):
+            passes = range(F // 512 if name == "st" else PASSES)
+            made = [weight_piece(name, g, g in scalar_passes) for g in passes]
             return [x for x, _ in made] + [x for _, x in made]
 
         def copy_out(out, in_, on_vector):
@@ -111,53 +122,62 @@ def tile_linear_state_step_s7_kernel(
             else:
                 nc.scalar.copy(out=out, in_=in_)
 
-        def load_scales():
-            nc.sync.dma_start(out=scale_sb[:], in_=xq_scale.rearrange("o k -> (o k)").partition_broadcast(P))
-
-        def product_q(c):
-            def slot(s):
-                if s == 0:
-                    rows["q", c] = sb.tile([P, PACK, D], BF16, name=f"xq{c}", tag="xq_rows", bufs=2, align_bytes=64)
-                nc.vector.tensor_tensor(
-                    out=rows["q", c][:, s, :], in0=rows_q[c][:, s, :].bitcast(FP8), in1=scale_sb[:], op=ALU.mult
+        def widen_q(c):
+            def pair(h):
+                if h == 0:
+                    rows["q", c] = sb.tile([P, 2, PACK * D // 2], BF16, name=f"xq{c}", tag="xq_rows", bufs=2, align_bytes=64)
+                half = PACK * D // 4
+                nc.vector.tensor_scalar(
+                    out=rows["q", c][:, :, h * half : (h + 1) * half].rearrange("p u (m e) -> p m u e", e=2),
+                    in0=rows_q[c][:, 2 * h : 2 * h + 2, :].bitcast(FP8).rearrange("p s (m u e) -> p (s m) u e", u=2, e=2),
+                    scalar1=ones[:, 0:1], scalar2=None, op0=ALU.mult,
                 )
 
-            return [lambda: slot(0), lambda: slot(1), lambda: slot(2), lambda: slot(3)]
+            return [lambda: pair(0), lambda: pair(1)]
 
-        def transpose_unit(kind, c, slots=(0, 1, 2, 3), on_vector=(0, 0, 0, 0)):
+        def transpose_pair(kind, c, h):
             t = rows[kind, c]
-            pend = []
-            for s in slots:
+            width = PASSES * P * PACK
+            grouped = sb.tile([P, 2 * width], BF16, name=f"g{kind}{c}{h}", tag="x_grouped", bufs=3, align_bytes=64)
+            for i in range(2):
+                s = 2 * h + i
                 bank = ps.tile([P, 512], F32, name=f"t{kind}{c}{s}", tag="bank")
-                bank4 = bank[:].rearrange("p (g u m) -> p g u m", g=PASSES, u=2)
-                words = t[:, s, :].bitcast(F32)
+                if kind == "q":
+                    bank4 = bank[:].rearrange("p (u g m) -> p g u m", g=PASSES, u=2)
+                else:
+                    bank4 = bank[:].rearrange("p (g u m) -> p g u m", g=PASSES, u=2)
                 for g in range(PASSES):
                     for u in range(2):
-                        nc.tensor.transpose(bank4[:, g, u, :], words[:, 256 * g + u : 256 * (g + 1) : 2], ident[:])
-                grouped = sb.tile([P, PASSES * P * PACK], BF16, name=f"g{kind}{c}{s}", tag="x_grouped", bufs=6, align_bytes=64)
-                copy_out(
-                    grouped[:].bitcast(F32).rearrange("p (g m u) -> p g m u", g=PASSES, u=2),
-                    bank4.rearrange("p g u m -> p g m u"),
-                    on_vector=on_vector[s],
-                )
-                codes = sb.tile([P, PASSES * P], U32, name=f"c{kind}{c}{s}", tag="x_codes", bufs=12, align_bytes=64)
-                scales = sb.tile([P, PASSES * P], U8, name=f"s{kind}{c}{s}", tag="x_scales", bufs=12, align_bytes=64)
-                xcodes[kind, c, s] = (codes, scales)
-                pend.append((codes, scales, grouped))
-                if len(pend) > 1:
-                    quant_x(*pend[-2])
-            quant_x(*pend[-1])
-
-        def quant_x(codes, scales, grouped):
+                        if kind == "q":
+                            first = s * PASSES * P + g * P
+                            chosen = t[:, u, :].bitcast(F32)[:, first : first + P]
+                        else:
+                            chosen = t[:, s, :].bitcast(F32)[:, 256 * g + u : 256 * (g + 1) : 2]
+                        nc.tensor.transpose(bank4[:, g, u, :], chosen, ident[:])
+                if kind == "q":
+                    nc.vector.tensor_tensor(
+                        out=grouped[:, i * width : (i + 1) * width].rearrange("p (g m u e) -> p g m u e", g=PASSES, u=2, e=2),
+                        in0=bank[:].bitcast(BF16).rearrange("p (u g m e) -> p g m u e", g=PASSES, u=2, e=2),
+                        in1=scale_pt[:].rearrange("p g (u e) -> p g u e", u=2).unsqueeze(2).to_broadcast([P, PASSES, P, 2, 2]),
+                        op=ALU.mult,
+                    )
+                else:
+                    nc.scalar.copy(
+                        out=grouped[:, i * width : (i + 1) * width].bitcast(F32).rearrange("p (g m u) -> p g m u", g=PASSES, u=2),
+                        in_=bank4.rearrange("p g u m -> p g m u"),
+                    )
+            codes, scales = new_operand(f"x{kind}{c}{h}", 2 * PASSES * P, "x", 6)
+            xcodes[kind, c, h] = (codes, scales)
             nc.vector.quantize_mx(out=codes[:].bitcast(FP8X4), scales=scales[:], in_=grouped[:])
 
         def x_operand(kind, c, s, g):
-            codes, scales = xcodes[kind, c, s]
-            cols = slice(g * P, (g + 1) * P)
-            return codes[:, cols].bitcast(FP8X4), scales[:, cols]
+            codes, scales = xcodes[kind, c, s // 2]
+            first = (s % 2) * PASSES * P + g * P
+            return codes[:, first : first + P].bitcast(FP8X4), scales[:, first : first + P]
 
         def w_operand(name, g, h, a, b):
-            codes, scales = wcodes[name, g, h]
+            codes, scales = wcodes[name, g]
+            a, b = a + h * HALF, b + h * HALF
             return codes[:, a:b].bitcast(FP8X4), scales[:, a:b]
 
         kcodes, vcodes, qcodes = {}, {}, {}
@@ -218,7 +238,7 @@ def tile_linear_state_step_s7_kernel(
                     copy_out(
                         grouped[:].rearrange("p (n s) -> p n s", s=PACK)[:, q * P : (q + 1) * P, :],
                         bank[:].rearrange("p (s n) -> p n s", s=PACK),
-                        on_vector=(q == 3),
+                        on_vector=False,
                     )
                 if q == 3:
                     codes, scales = vcodes[c, h]
@@ -274,7 +294,7 @@ def tile_linear_state_step_s7_kernel(
                         out=bank[:], lhsT=codes[:, cols].bitcast(FP8X4), lhsT_scale=scales[:, cols],
                         rhs=rhs, rhs_scale=rhs_s, start=True, stop=True,
                     )
-                    copy_out(o_sb[:, h * HALF : (h + 1) * HALF], bank[:], on_vector=(c == 1 and h == 1))
+                    copy_out(o_sb[:, h * HALF : (h + 1) * HALF], bank[:], on_vector=False)
                 if c == CHUNKS - 1:
                     cut = slice(h * HALF, (h + 1) * HALF)
                     nc.sync.dma_start(out=out_view[c, :, s, cut], in_=o_sb[:, cut])
@@ -336,73 +356,75 @@ def tile_linear_state_step_s7_kernel(
                         fill(arg)
 
         with tc.manual_schedule(engines={mybir.EngineType.PE}):
-            transpose_unit("k", 0)
-            for job in weights("wk", ((0, 0), (1, 0)), ((1, 0),)):
+            transpose_pair("k", 0, 0)
+            transpose_pair("k", 0, 1)
+            for job in weights("wk"):
                 job()
-            load_w("wv", wv)
+            load_w("wv", wv, (0,))
+            load_x("k", 2)
+            load_w("wv", wv, (1,))
             load_x("v", 0)
             load_x("v", 1)
             load_scales()
             load_x("q", 0)
-            background.extend(weights("wv", ((0, 0), (1, 0))))
-            background.extend(weights("wv", ((0, 1), (1, 1))))
-            background.extend(product_q(0))
-            transpose_unit("k", 1, (0, 1))
-            k = project_k(0)
-            spread(k[:2], 1)
-            transpose_unit("k", 1, (2, 3))
-            spread(k[2:], 1)
+            background.extend(weights("wv"))
+            background.extend(widen_q(0))
+            transpose_pair("k", 1, 0)
+            fills = project_k(0)
+            spread(fills[:2], 1)
+            transpose_pair("k", 1, 1)
+            spread(fills[2:], 1)
             load_w("wq", wq)
             load_x("q", 1)
             load_w("st", state)
             nc.sync.dma_start(out=decay_sb[:], in_=decay.rearrange("(p i) -> p i", i=PACK))
             load_x("v", 2)
+            background.extend(weights("wq"))
+            background.extend(widen_q(1))
+            background.extend(weights("st"))
+            background.extend(widen_q(2))
+            transpose_pair("k", 2, 0)
+            fills = project_k(1)
+            spread(fills[:2], 2)
+            transpose_pair("k", 2, 1)
+            spread(fills[2:], 1)
+            transpose_pair("v", 0, 0)
+            fills = project_k(2)
+            spread(fills[:2], 2)
+            transpose_pair("v", 0, 1)
+            spread(fills[2:], 3)
+            transpose_pair("v", 1, 0)
+            fills = project_v(0)
+            spread(fills[:4], 2)
+            transpose_pair("v", 1, 1)
+            spread(fills[4:], 0)
             load_x("q", 2)
-            background.extend(weights("wq", ((0, 0), (1, 0))))
-            background.extend(product_q(1))
-            background.extend(weights("st", ((0, 0), (0, 1))))
-            background.extend(product_q(2))
-            transpose_unit("k", 2, (0, 1))
-            k = project_k(1)
-            spread(k[:2], 2)
-            transpose_unit("k", 2, (2, 3))
-            spread(k[2:], 3)
-            transpose_unit("v", 0, (0, 1))
-            k = project_k(2)
-            spread(k[:2], 3)
-            transpose_unit("v", 0, (2, 3))
-            spread(k[2:], 2)
-            transpose_unit("v", 1, (0, 1))
-            v = project_v(0)
-            spread(v[:4], 2)
-            transpose_unit("v", 1, (2, 3))
-            spread(v[4:], 2)
-            transpose_unit("q", 0, (0, 1))
-            v = project_v(1)
-            spread(v[:4], 3)
-            transpose_unit("q", 0, (2, 3))
-            spread(v[4:], 3)
-            transpose_unit("q", 1, (0, 1))
-            q = project_q(0)
-            spread(q[:2], 2)
-            transpose_unit("q", 1, (2, 3))
-            spread(q[2:], 2)
-            transpose_unit("v", 2, (0, 1))
-            q = project_q(1)
+            transpose_pair("q", 0, 0)
+            fills = project_v(1)
+            spread(fills[:4], 0)
+            transpose_pair("q", 0, 1)
+            spread(fills[4:], 1)
+            transpose_pair("v", 2, 0)
+            fills = project_q(0)
+            spread(fills[:2], 0)
+            transpose_pair("v", 2, 1)
+            spread(fills[2:], 1)
+            transpose_pair("q", 1, 0)
+            fills = project_v(2)
             read = read_state(0)
-            spread(mix(q[:2], read[:2]) + read[2:4], 2)
-            transpose_unit("v", 2, (2, 3))
-            spread(mix(q[2:], read[4:6]) + read[6:], 2)
-            transpose_unit("q", 2, (0, 1))
-            v = project_v(2)
-            read = read_state(1)
-            run(v[:4], read[:4])
-            transpose_unit("q", 2, (2, 3))
-            run(v[4:], read[4:])
+            spread(mix(fills[:4], read[:4]), 1)
+            transpose_pair("q", 1, 1)
+            spread(mix(fills[4:], read[4:]), 1)
+            transpose_pair("q", 2, 0)
+            fills = project_q(1)
+            spread(fills[:2], 0)
+            transpose_pair("q", 2, 1)
+            spread(fills[2:], 0)
             update = update_state(0) + update_state(1)
-            run(project_q(2), update[:2])
+            read = read_state(1)
+            run(read[:4], update[:2])
+            run(project_q(2), read[4:])
+            run(update[2:3])
             read = read_state(2)
-            run(update[2:4], read[:2])
-            run(read[2:6])
-            run(update[4:6], read[6:])
-            run(update[6:])
+            run(read, update[3:5])
+            run(update[5:])

from contextlib import ExitStack

import concourse.mybir as mybir
from concourse.masks import make_identity

T, D, F, E = 1536, 1024, 512, 1024
FLOPS = 2 * T * (2 * D * F + D * E + 2 * F * E)

F32 = mybir.dt.float32
BF16 = mybir.dt.bfloat16
U32 = mybir.dt.uint32
U8 = mybir.dt.uint8
FP8 = mybir.dt.float8_e4m3fn
FP8X4 = mybir.dt.float8_e4m3fn_x4
ACT = mybir.ActivationFunctionType
ALU = mybir.AluOpType

P = 128
PACK = 4
CHUNK = 512
CHUNKS = T // CHUNK
PASSES = D // 512
HALF = 512


def tile_linear_state_step_s7_kernel(
    tc, xq_bytes, xq_scale, xk, xv, wq, wk, wv, state, decay, out_0, out_1
):
    nc = tc.nc

    with ExitStack() as ctx:
        sb = ctx.enter_context(tc.tile_pool(name="sb", bufs=1))
        ps = ctx.enter_context(tc.psum_pool(name="ps", bufs=8))

        ident = sb.tile([P, P], F32, name="ident", align_bytes=64)
        make_identity(nc, ident[:])

        decay_sb = sb.tile([P, PACK], BF16, name="decay_sb")
        warm = sb.tile([P, 1], F32, name="warm")
        nc.vector.memset(warm[:], 0.0)
        nc.scalar.activation(out=warm[:], in_=warm[:], func=ACT.Relu)

        xdram = {"k": xk, "v": xv, "q": xq_bytes}
        rows = {}
        rows_q = {}
        xcodes = {}

        def load_x(kind, c, cuts=(0, 4)):
            view = xdram[kind][c * CHUNK : (c + 1) * CHUNK, :].rearrange("(m s) d -> m s d", s=PACK)
            if kind == "q":
                t = sb.tile([P, PACK, D], U8, name=f"xqb{c}", tag="xq_bytes", bufs=2, align_bytes=64)
                rows_q[c] = t
            else:
                if cuts[0] == 0:
                    rows[kind, c] = sb.tile([P, PACK, D], BF16, name=f"x{kind}{c}", tag="x_rows", bufs=4, align_bytes=64)
                t = rows[kind, c]
            for a, b in zip(cuts[:-1], cuts[1:]):
                nc.sync.dma_start(out=t[:, a:b, :], in_=view[:, a:b, :])

        scale_pt = sb.tile([P, PASSES, PACK], F32, name="scale_pt", align_bytes=64)
        ones = sb.tile([P, 1], F32, name="ones")
        nc.vector.memset(ones[:], 1.0)

        def load_scales():
            nc.sync.dma_start(out=scale_pt[:], in_=xq_scale.rearrange("o (g p t) -> p (o g) t", p=P, t=PACK))

        wraw = {}

        def load_w(name, w, passes=None):
            width = w.shape[1]
            for g in passes or range(w.shape[0] // 512):
                if name in ("wk", "wq"):
                    t = sb.tile([P, PACK, width], BF16, name=f"{name}raw{g}", tag="w_small", bufs=2, align_bytes=64)
                else:
                    t = sb.tile([P, PACK, width], BF16, name=f"{name}raw{g}", align_bytes=64)
                nc.sync.dma_start(out=t[:], in_=w[512 * g : 512 * (g + 1), :].rearrange("(p j) n -> p j n", j=PACK))
                wraw[name, g] = t

        load_x("k", 0, (0, 2))
        load_w("wk", wk, (0,))
        load_x("k", 0, (2, 4))
        load_w("wk", wk, (1,))
        load_x("k", 1, (0, 2))
        load_x("k", 1, (2, 4))

        wcodes = {}

        def weight_piece(name, g, on_scalar=False):
            raw = wraw[name, g]
            width = raw.shape[2]
            grouped = sb.tile([P, width * PACK], BF16, name=f"{name}g{g}", tag="w_grouped", bufs=2, align_bytes=64)
            codes = sb.tile([P, width], U32, name=f"{name}c{g}", align_bytes=64)
            scales = sb.tile([P, width], U8, name=f"{name}s{g}", align_bytes=64)
            wcodes[name, g] = (codes, scales)

            def interleave():
                if name == "wq":
                    nc.vector.tensor_copy(
                        out=grouped[:].rearrange("p (t m j) -> p t m j", t=PACK, j=PACK),
                        in_=raw[:].rearrange("p j (m t) -> p t m j", t=PACK),
                    )
                else:
                    copy_out(
                        grouped[:].rearrange("p (c i j) -> p c j i", i=4, j=PACK),
                        raw[:].rearrange("p j (c i) -> p c j i", i=4),
                        on_vector=not on_scalar,
                    )

            def quant():
                nc.vector.quantize_mx(out=codes[:].bitcast(FP8X4), scales=scales[:], in_=grouped[:])

            return interleave, quant

        def weights(name, scalar_passes=()):
            passes = range(F // 512 if name == "st" else PASSES)
            made = [weight_piece(name, g, g in scalar_passes) for g in passes]
            return [x for x, _ in made] + [x for _, x in made]

        def copy_out(out, in_, on_vector):
            if on_vector:
                nc.vector.tensor_copy(out=out, in_=in_)
            else:
                nc.scalar.copy(out=out, in_=in_)

        def widen_q(c):
            def pair(h):
                if h == 0:
                    rows["q", c] = sb.tile([P, 2, PACK * D // 2], BF16, name=f"xq{c}", tag="xq_rows", bufs=2, align_bytes=64)
                half = PACK * D // 4
                nc.vector.tensor_scalar(
                    out=rows["q", c][:, :, h * half : (h + 1) * half].rearrange("p u (m e) -> p m u e", e=2),
                    in0=rows_q[c][:, 2 * h : 2 * h + 2, :].bitcast(FP8).rearrange("p s (m u e) -> p (s m) u e", u=2, e=2),
                    scalar1=ones[:, 0:1], scalar2=None, op0=ALU.mult,
                )

            return [lambda: pair(0), lambda: pair(1)]

        def transpose_pair(kind, c, h):
            t = rows[kind, c]
            width = PASSES * P * PACK
            grouped = sb.tile([P, 2 * width], BF16, name=f"g{kind}{c}{h}", tag="x_grouped", bufs=3, align_bytes=64)
            for i in range(2):
                s = 2 * h + i
                bank = ps.tile([P, 512], F32, name=f"t{kind}{c}{s}", tag="bank")
                if kind == "q":
                    bank4 = bank[:].rearrange("p (u g m) -> p g u m", g=PASSES, u=2)
                else:
                    bank4 = bank[:].rearrange("p (g u m) -> p g u m", g=PASSES, u=2)
                for g in range(PASSES):
                    for u in range(2):
                        if kind == "q":
                            first = s * PASSES * P + g * P
                            chosen = t[:, u, :].bitcast(F32)[:, first : first + P]
                        else:
                            chosen = t[:, s, :].bitcast(F32)[:, 256 * g + u : 256 * (g + 1) : 2]
                        nc.tensor.transpose(bank4[:, g, u, :], chosen, ident[:])
                if kind == "q":
                    nc.vector.tensor_tensor(
                        out=grouped[:, i * width : (i + 1) * width].rearrange("p (g m u e) -> p g m u e", g=PASSES, u=2, e=2),
                        in0=bank[:].bitcast(BF16).rearrange("p (u g m e) -> p g m u e", g=PASSES, u=2, e=2),
                        in1=scale_pt[:].rearrange("p g (u e) -> p g u e", u=2).unsqueeze(2).to_broadcast([P, PASSES, P, 2, 2]),
                        op=ALU.mult,
                    )
                else:
                    nc.scalar.copy(
                        out=grouped[:, i * width : (i + 1) * width].bitcast(F32).rearrange("p (g m u) -> p g m u", g=PASSES, u=2),
                        in_=bank4.rearrange("p g u m -> p g m u"),
                    )
            codes, scales = new_operand(f"x{kind}{c}{h}", 2 * PASSES * P, "x", 6)
            xcodes[kind, c, h] = (codes, scales)
            nc.vector.quantize_mx(out=codes[:].bitcast(FP8X4), scales=scales[:], in_=grouped[:])

        def x_operand(kind, c, s, g):
            codes, scales = xcodes[kind, c, s // 2]
            first = (s % 2) * PASSES * P + g * P
            return codes[:, first : first + P].bitcast(FP8X4), scales[:, first : first + P]

        def w_operand(name, g, h, a, b):
            codes, scales = wcodes[name, g]
            a, b = a + h * HALF, b + h * HALF
            return codes[:, a:b].bitcast(FP8X4), scales[:, a:b]

        kcodes, vcodes, qcodes = {}, {}, {}

        def new_operand(name, words, tag, bufs):
            codes = sb.tile([P, words], U32, name=f"{name}_codes", tag=f"{tag}_codes", bufs=bufs, align_bytes=64)
            scales = sb.tile([P, words], U8, name=f"{name}_scales", tag=f"{tag}_scales", bufs=bufs, align_bytes=64)
            return codes, scales

        def grouped_tile(name):
            return sb.tile([P, 2048], BF16, name=name, tag="y_grouped", bufs=4, align_bytes=64)

        def project_k(c):
            grouped = grouped_tile(f"kg{c}")
            kcodes[c] = new_operand(f"k{c}", F, "k", 3)

            def fill(q):
                bank = ps.tile([P, 512], F32, name=f"kb{c}{q}", tag="bank")
                for s in range(PACK):
                    for g in range(PASSES):
                        lhs, lhs_s = x_operand("k", c, s, g)
                        rhs, rhs_s = w_operand("wk", g, 0, q * P, (q + 1) * P)
                        nc.tensor.matmul_mx(
                            out=bank[:, s * P : (s + 1) * P], lhsT=lhs, lhsT_scale=lhs_s, rhs=rhs, rhs_scale=rhs_s,
                            start=(g == 0), stop=(g == PASSES - 1),
                        )
                nc.scalar.activation(
                    out=grouped[:].rearrange("p (i m s) -> p i m s", i=PACK, s=PACK)[:, :, 32 * q : 32 * q + 32, :],
                    in_=bank[:].rearrange("p (s m i) -> p i m s", s=PACK, i=PACK),
                    func=ACT.Relu,
                )
                if q == 3:
                    codes, scales = kcodes[c]
                    nc.vector.quantize_mx(out=codes[:].bitcast(FP8X4), scales=scales[:], in_=grouped[:])

            return [(fill, q) for q in range(4)]

        def project_v(c):
            halves = {}

            def fill(n):
                h, q = n // 4, n % 4
                if q == 0:
                    grouped = grouped_tile(f"vg{c}{h}")
                    halves[h] = grouped
                    vcodes[c, h] = new_operand(f"v{c}{h}", HALF, "v", 6)
                grouped = halves[h]
                if True:
                    bank = ps.tile([P, 512], F32, name=f"vb{c}{h}{q}", tag="bank")
                    for s in range(PACK):
                        for g in range(PASSES):
                            lhs, lhs_s = x_operand("v", c, s, g)
                            rhs, rhs_s = w_operand("wv", g, h, q * P, (q + 1) * P)
                            nc.tensor.matmul_mx(
                                out=bank[:, s * P : (s + 1) * P], lhsT=lhs, lhsT_scale=lhs_s, rhs=rhs, rhs_scale=rhs_s,
                                start=(g == 0), stop=(g == PASSES - 1),
                            )
                    copy_out(
                        grouped[:].rearrange("p (n s) -> p n s", s=PACK)[:, q * P : (q + 1) * P, :],
                        bank[:].rearrange("p (s n) -> p n s", s=PACK),
                        on_vector=False,
                    )
                if q == 3:
                    codes, scales = vcodes[c, h]
                    nc.vector.quantize_mx(out=codes[:].bitcast(FP8X4), scales=scales[:], in_=grouped[:])

            return [(fill, n) for n in range(8)]

        def project_q(c):
            grouped = grouped_tile(f"qg{c}")

            def fill(s):
                bank = ps.tile([P, 512], F32, name=f"qb{c}{s}", tag="bank")
                for j in range(PACK):
                    for g in range(PASSES):
                        lhs, lhs_s = w_operand("wq", g, 0, j * P, (j + 1) * P)
                        rhs, rhs_s = x_operand("q", c, s, g)
                        nc.tensor.matmul_mx(
                            out=bank[:, j * P : (j + 1) * P], lhsT=lhs, lhsT_scale=lhs_s, rhs=rhs, rhs_scale=rhs_s,
                            start=(g == 0), stop=(g == PASSES - 1),
                        )
                copy_out(
                    grouped[:, s * 512 : (s + 1) * 512].rearrange("p (m j) -> p m j", j=PACK),
                    bank[:].rearrange("p (j m) -> p m j", j=PACK),
                    on_vector=False,
                )
                if s % 2 == 1:
                    pair = s // 2
                    qcodes[c, pair] = new_operand(f"q{c}{pair}", 2 * P, "q", 4)
                    codes, scales = qcodes[c, pair]
                    nc.vector.quantize_mx(
                        out=codes[:].bitcast(FP8X4), scales=scales[:], in_=grouped[:, pair * 1024 : (pair + 1) * 1024]
                    )

            return [(fill, s) for s in range(PACK)]

        out_view = out_0.rearrange("(c m s) e -> c m s e", m=P, s=PACK)

        def read_state(c):
            row_tiles = {}

            def fill(n):
                s, h = n // 2, n % 2
                codes, scales = qcodes[c, s // 2]
                cols = slice((s % 2) * P, (s % 2 + 1) * P)
                if h == 0:
                    o_sb = sb.tile([P, E], F32, name=f"o{c}{s}", tag="out_rows", bufs=4)
                    row_tiles[s] = o_sb
                o_sb = row_tiles[s]
                if True:
                    bank = ps.tile([P, 512], F32, name=f"ob{c}{s}{h}", tag="bank")
                    rhs, rhs_s = w_operand("st", 0, h, 0, HALF)
                    nc.tensor.matmul_mx(
                        out=bank[:], lhsT=codes[:, cols].bitcast(FP8X4), lhsT_scale=scales[:, cols],
                        rhs=rhs, rhs_scale=rhs_s, start=True, stop=True,
                    )
                    copy_out(o_sb[:, h * HALF : (h + 1) * HALF], bank[:], on_vector=False)
                if c == CHUNKS - 1:
                    cut = slice(h * HALF, (h + 1) * HALF)
                    nc.sync.dma_start(out=out_view[c, :, s, cut], in_=o_sb[:, cut])
                elif h == 1:
                    nc.sync.dma_start(out=out_view[c, :, s, :], in_=o_sb[:])

            return [(fill, n) for n in range(8)]

        new_view = out_1.rearrange("(p i) e -> p i e", i=PACK)

        def update_state(h):
            banks = {}

            def passes(i, chunks):
                for c in chunks:
                    codes, scales = kcodes[c]
                    vc, vs = vcodes[c, h]
                    cols = slice(i * P, (i + 1) * P)
                    nc.tensor.matmul_mx(
                        out=banks[i][:], lhsT=codes[:, cols].bitcast(FP8X4), lhsT_scale=scales[:, cols],
                        rhs=vc[:].bitcast(FP8X4), rhs_scale=vs[:], start=(c == 0), stop=(c == 2),
                    )

            def fill(i):
                bank = ps.tile([P, 512], F32, name=f"ub{h}{i}", tag="bank")
                banks[i] = bank
                passes(i, (0, 1, 2))
                new_sb = sb.tile([P, HALF], F32, name=f"n{h}{i}", tag="new_rows", bufs=4)
                cut = slice(h * HALF, (h + 1) * HALF)
                nc.vector.scalar_tensor_tensor(
                    out=new_sb[:], in0=wraw["st", 0][:, i, cut], scalar=decay_sb[:, i : i + 1], in1=bank[:],
                    op0=ALU.mult, op1=ALU.add,
                )
                nc.sync.dma_start(out=new_view[:, i, cut], in_=new_sb[:])

            return [(fill, i) for i in range(PACK)]

        background = []

        def work(n):
            for _ in range(min(n, len(background))):
                job = background[0]
                background.remove(job)
                job()

        def spread(fills, n):
            for i, (fill, arg) in enumerate(fills):
                work((i + 1) * n // len(fills) - i * n // len(fills))
                fill(arg)

        def mix(a, b):
            return [x for pair in zip(a, b) for x in pair]

        def run(*lists):
            for n in range(max(len(x) for x in lists)):
                for x in lists:
                    if n < len(x):
                        fill, arg = x[n]
                        fill(arg)

        with tc.manual_schedule(engines={mybir.EngineType.PE}):
            transpose_pair("k", 0, 0)
            transpose_pair("k", 0, 1)
            for job in weights("wk"):
                job()
            load_w("wv", wv, (0,))
            load_x("k", 2)
            load_w("wv", wv, (1,))
            load_x("v", 0)
            load_x("v", 1)
            load_scales()
            load_x("q", 0)
            background.extend(weights("wv"))
            background.extend(widen_q(0))
            transpose_pair("k", 1, 0)
            fills = project_k(0)
            spread(fills[:2], 1)
            transpose_pair("k", 1, 1)
            spread(fills[2:], 1)
            load_w("wq", wq)
            load_x("q", 1)
            load_w("st", state)
            nc.sync.dma_start(out=decay_sb[:], in_=decay.rearrange("(p i) -> p i", i=PACK))
            load_x("v", 2)
            background.extend(weights("wq"))
            background.extend(widen_q(1))
            background.extend(weights("st"))
            background.extend(widen_q(2))
            transpose_pair("k", 2, 0)
            fills = project_k(1)
            spread(fills[:2], 2)
            transpose_pair("k", 2, 1)
            spread(fills[2:], 1)
            transpose_pair("v", 0, 0)
            fills = project_k(2)
            spread(fills[:2], 2)
            transpose_pair("v", 0, 1)
            spread(fills[2:], 3)
            transpose_pair("v", 1, 0)
            fills = project_v(0)
            spread(fills[:4], 2)
            transpose_pair("v", 1, 1)
            spread(fills[4:], 0)
            load_x("q", 2)
            transpose_pair("q", 0, 0)
            fills = project_v(1)
            spread(fills[:4], 0)
            transpose_pair("q", 0, 1)
            spread(fills[4:], 1)
            transpose_pair("v", 2, 0)
            fills = project_q(0)
            spread(fills[:2], 0)
            transpose_pair("v", 2, 1)
            spread(fills[2:], 1)
            transpose_pair("q", 1, 0)
            fills = project_v(2)
            read = read_state(0)
            spread(mix(fills[:4], read[:4]), 1)
            transpose_pair("q", 1, 1)
            spread(mix(fills[4:], read[4:]), 1)
            transpose_pair("q", 2, 0)
            fills = project_q(1)
            spread(fills[:2], 0)
            transpose_pair("q", 2, 1)
            spread(fills[2:], 0)
            update = update_state(0) + update_state(1)
            read = read_state(1)
            run(read[:4], update[:2])
            run(project_q(2), read[4:])
            run(update[2:3])
            read = read_state(2)
            run(read, update[3:5])
            run(update[5:])
